import numpy as np, ml_dtypes
CORES = [56,64,184,192,312,320,440,448]
N = 8
KB, QP = 1, 64
ROOT = 3
def setup_inputs(rng):
    q = rng.standard_normal((N, 128, QP), dtype=np.float32) / 4; k = rng.standard_normal((N, 128, KB * 128), dtype=np.float32)
    a = 2 * np.pi * rng.random((N, QP)); s = 400 * rng.random((N, QP)) ** 1.5; q[:, 0, :] = s * np.cos(a); q[:, 1, :] = s * np.sin(a); q[:, 2, :] = 150 * rng.standard_normal((N, QP)); k[:, 2, :] = 1 + k[:, 2, :] / 50
    a = (2 * np.pi * rng.random() + np.pi / 2 * (rng.permutation(N).reshape(N, 1, 1) + 0.5) / N - 0.5 + (np.arange(KB).reshape(1, KB, 1) + rng.random((N, KB, 128))) / KB).reshape(N, KB * 128); k[:, 0, :] = np.cos(a); k[:, 1, :] = np.sin(a)
    for t in range(0, QP, 2):
        j, i = (t // 2) % N, rng.integers(KB * 128); q[ROOT, :2, t] = s[ROOT, t] * k[j, :2, i]; q[ROOT, 3:, t] += k[j, 3:, i] / 8
    return {"q": q.astype(ml_dtypes.bfloat16), "k": k.astype(ml_dtypes.bfloat16), "v": rng.standard_normal((N, 128, KB * 128), dtype=np.float32).astype(ml_dtypes.bfloat16)}
def setup_inputs_big(rng):
    d = setup_inputs(rng)
    for k in ("v",): d[k] = (d[k].astype(np.float32) * 1048576.0).astype(d[k].dtype)
    return d
def setup_inputs_small(rng):
    d = setup_inputs(rng)
    for k in ("v",): d[k] = (d[k].astype(np.float32) * (1 / 1048576.0)).astype(d[k].dtype)
    return d
def reference(q, k, v):
    Q, K, V = q.astype(np.float64), k.astype(np.float64), v.astype(np.float64)
    y = np.full((N, QP, 128), np.nan)
    for r in [ROOT]:
        js = list(range(N))
        S = np.concatenate([K[j].T @ Q[r] for j in js], axis=0)
        P = np.exp(S - S.max(axis=0)); P = P / P.sum(axis=0)
        y[r] = P.T @ np.concatenate([V[j][:, 128 * b:128 * b + 128] for j in js for b in range(KB)], axis=0)
    return {"y": y.astype(ml_dtypes.bfloat16)}

@@ -1,0 +1,291 @@
+from concourse.mybir import AluOpType, AxisListType, ActivationFunctionType
+
+NEV = 80
+ENG_HOP = 8
+ENG_ROOT = 8
+
+SCRATCH = {
+    "stg": ("dram", [2, 128, 128], "bfloat16"),
+    "qs": ("sbuf", [128, 64], "bfloat16"),
+    "K": ("sbuf", [128, 1024], "bfloat16"),
+    "V": ("sbuf", [128, 1024], "bfloat16"),
+    "ident": ("sbuf", [128, 64], "bfloat16"),
+    "pT": ("sbuf", [128, 1024], "bfloat16"),
+    "P": ("sbuf", [128, 512], "bfloat16"),
+    "Oa": ("sbuf", [128, 128], "bfloat16"),
+    "Ob": ("sbuf", [128, 128], "bfloat16"),
+    "Da": ("sbuf", [128, 64], "bfloat16"),
+    "Db": ("sbuf", [128, 64], "bfloat16"),
+    "nm": ("sbuf", [128, 16], "float32"),
+    "sl": ("sbuf", [128, 24], "float32"),
+    "ysb": ("sbuf", [128, 128], "bfloat16"),
+    "ST0": ("psum", [128, 512], "float32"), "ST1": ("psum", [128, 512], "float32"), "ST2": ("psum", [128, 512], "float32"),
+    "PT0": ("psum", [128, 1024], "bfloat16"), "PT1": ("psum", [128, 1024], "bfloat16"), "PT2": ("psum", [128, 1024], "bfloat16"),
+    "O0": ("psum", [128, 512], "float32"), "O1": ("psum", [128, 512], "float32"),
+}
+SEMAPHORES = (["lq", "lk", "lv", "snt", "rk", "rv", "sty"] + ["ka%d" % j for j in range(8)] + ["va%d" % j for j in range(8)]
+              + ["e%d" % i for i in range(NEV)])
+
+PLANS = {}
+
+
+def plan(T, topo):
+    if "plan" not in PLANS:
+        PLANS["plan"] = make_plan(T, topo)
+    return PLANS["plan"]
+
+
+def make_plan(T, topo):
+    group = list(T.cores)
+    root = group[T.root]
+    per_host = topo.CORES_PER_HOST
+    world = range((1 + max(topo.host(c) for c in group)) * per_host)
+    mate_of = {}
+
+    def chipof(c):
+        return (topo.host(c), topo.chip(c))
+
+    def inrack(a, b):
+        if chipof(a) == chipof(b):
+            return []
+        d = topo.die(a)
+        if topo.mates(a, b):
+            return [("mate", chipof(a), d)]
+        if topo.same_plane(a, b):
+            return [("out", chipof(a), d), ("in", chipof(b), d)]
+        if chipof(a) not in mate_of:
+            mate_of[chipof(a)] = [x for x in world if topo.mates(a, x)][0]
+        m = mate_of[chipof(a)]
+        return [("mate", chipof(a), d), ("out", chipof(m), d), ("in", chipof(b), d)]
+
+    def links(a, b):
+        if topo.rack(topo.host(a)) == topo.rack(topo.host(b)):
+            return inrack(a, b)
+        shift = (topo.host(b) - topo.host(a)) * per_host
+        d = topo.die(a)
+        return [("cable", chipof(a), d)] + inrack(a + shift, b) + inrack(a, b - shift) + [("cable", chipof(b - shift), d)]
+
+    direct = [c for c in group if c != root and topo.may_write(c, root)]
+    far = [c for c in group if c != root and not topo.may_write(c, root)]
+    relay, busy = {}, []
+    for r in far:
+        cand = [c for c in world if c not in group and c not in relay.values()
+                and topo.may_write(r, c) and topo.may_write(c, root)]
+        best, best_cost = None, None
+        for c in cand:
+            way = links(r, c) + links(c, root)
+            cost = (len([x for x in way if x in busy]), len(set(way)), topo.die(c) != topo.die(r), -c)
+            if best is None or cost < best_cost:
+                best, best_cost = c, cost
+        relay[r] = best
+        busy += links(r, best) + links(best, root)
+    return root, direct, far, relay
+
+
+def engines(mask, n):
+    out, bit = 0, 1
+    while n > 0:
+        if mask & bit:
+            out |= bit
+            n -= 1
+        bit <<= 1
+    return out
+
+
+def send(g, T, topo, core, dst, out_ap, in_ap, sem, n):
+    rid, pid = topo.addr(dst, core)
+    g.remote_dma(out_ap=out_ap, in_ap=in_ap, remote_sem=sem, local_sem=T.sem.snt, pid=pid, routing_id=rid,
+                 dma_engine_mask=engines(topo.mask(core, dst), n))
+
+
+def rank_program(g, core, T, topo):
+    root, direct, far, relay = plan(T, topo)
+    order = [root] + direct + far
+    if core == root:
+        n0, n1 = 1, 1 + len(direct)
+        late = list(range(n1, len(order)))
+        chunks = [late[0:1], late[1:3], late[3:5]]
+        root_program(g, T, [T.rank_of(c) for c in order], [[[0]], [list(range(n0, n1))], chunks])
+        return
+    if core in order:
+        b, j = order.index(core), T.rank_of(core)
+        g.sync.dma_start(T.stg[0], T.k[:, :]).then_inc(T.sem.lk, 16)
+        g.scalar.dma_start(T.stg[1], T.v[:, :]).then_inc(T.sem.lv, 16)
+        cols = slice(128 * b, 128 * b + 128)
+        if core in direct:
+            g.wait_ge(T.sem.lk, 16)
+            send(g, T, topo, core, root, T.K[:, cols], T.stg[0], T.sem["ka%d" % j], ENG_ROOT)
+            g.wait_ge(T.sem.lv, 16)
+            send(g, T, topo, core, root, T.V[:, cols], T.stg[1], T.sem["va%d" % j], ENG_ROOT)
+            g.wait_ge(T.sem.snt, 2 * ENG_ROOT)
+        else:
+            g.wait_ge(T.sem.lk, 16)
+            send(g, T, topo, core, relay[core], T.stg[0], T.stg[0], T.sem.rk, ENG_HOP)
+            g.wait_ge(T.sem.lv, 16)
+            send(g, T, topo, core, relay[core], T.stg[1], T.stg[1], T.sem.rv, ENG_HOP)
+            g.wait_ge(T.sem.snt, 2 * ENG_HOP)
+        return
+    for r in far:
+        if relay[r] == core:
+            b, j = order.index(r), T.rank_of(r)
+            cols = slice(128 * b, 128 * b + 128)
+            g.wait_ge(T.sem.rk, ENG_HOP)
+            send(g, T, topo, core, root, T.K[:, cols], T.stg[0], T.sem["ka%d" % j], ENG_ROOT)
+            g.wait_ge(T.sem.rv, ENG_HOP)
+            send(g, T, topo, core, root, T.V[:, cols], T.stg[1], T.sem["va%d" % j], ENG_ROOT)
+            g.wait_ge(T.sem.snt, 2 * ENG_ROOT)
+
+
+def root_program(g, T, rank_of_slot, stages):
+    A, X, F = AluOpType, AxisListType.X, ActivationFunctionType
+    pe, dve, act, sp = g.tensor, g.vector, g.scalar, g.sync
+    ST, PT, OB = [T.ST0, T.ST1, T.ST2], [T.PT0, T.PT1, T.PT2], [T.O0, T.O1]
+    QP = 64
+    count, need, open_ev = [0], {}, {}
+
+    def sig(*instrs):
+        name = "e%d" % count[0]
+        count[0] += 1
+        for ins in instrs:
+            ins.then_inc(T.sem[name], 1)
+        need[name] = len(instrs)
+        open_ev[name] = True
+        return name
+
+    def wait(queue, name):
+        queue.wait_ge(T.sem[name], need[name])
+        open_ev[name] = False
+
+    def col(t, c):
+        return t[0:QP, c:c + 1]
+
+    sp.dma_start(T.qs[:, :], T.q[:, :]).then_inc(T.sem.lq, 16)
+    act.dma_start(T.K[:, 0:128], T.k[:, :]).then_inc(T.sem.lk, 16)
+    sp.dma_start(T.V[:, 0:128], T.v[:, :]).then_inc(T.sem.lv, 16)
+    ones = sig(dve.memset(T.ident[0:QP, :], 1.0))
+    wait(g, ones)
+    idn = sig(g.affine_select(T.ident[0:QP, :], T.ident[0:QP, :], [[-1, QP]], A.is_equal, 0.0, 0, 1))
+    wait(pe, idn)
+    wait(dve, idn)
+    pe.wait_ge(T.sem.lq, 16)
+
+    def k_here(b):
+        if b == 0:
+            pe.wait_ge(T.sem.lk, 16)
+        else:
+            pe.wait_ge(T.sem["ka%d" % rank_of_slot[b]], ENG_ROOT)
+
+    def v_here(b):
+        if b == 0:
+            pe.wait_ge(T.sem.lv, 16)
+        else:
+            pe.wait_ge(T.sem["va%d" % rank_of_slot[b]], ENG_ROOT)
+
+    banks_of = [[0], [1], [2, 0, 1]]
+    keep = [(T.Oa, T.Da), (T.Ob, T.Db)]
+    nmc, slc = [0], [0]
+    prev = None
+    for s, chunks in enumerate(stages):
+        last = s == len(stages) - 1
+        banks, n, O = banks_of[s], len(chunks), OB[s % 2]
+        span = [(128 * ch[0], 128 * len(ch)) for ch in chunks]
+        st = []
+        for i, ch in enumerate(chunks):
+            for b in ch:
+                k_here(b)
+            c0, w = span[i]
+            st.append(sig(pe.matmul(ST[banks[i]][0:QP, 0:w], T.qs[:, :], T.K[:, c0:c0 + w], True, True)))
+        base = nmc[0]
+        red = []
+        for i in range(n):
+            wait(dve, st[i])
+            red.append(sig(dve.tensor_reduce(col(T.nm, base + i), ST[banks[i]][0:QP, 0:span[i][1]], X, A.max, negate=True)))
+        if prev is None and n == 1:
+            shift, shift_ev = base, red[0]
+        else:
+            for e in red:
+                wait(dve, e)
+            lo = base
+            if prev is not None:
+                wait(dve, prev["shift_ev"])
+                lo = base - 1
+            shift = base + n
+            shift_ev = sig(dve.tensor_reduce(col(T.nm, shift), T.nm[0:QP, lo:base + n], X, A.min))
+        nmc[0] = shift + 1
+        wait(act, shift_ev)
+        lc = slc[0]
+        wc, lsum, Lc, rc = lc + n, lc + n + 1, lc + n + 2, lc + n + 3
+        slc[0] = lc + n + 4
+        ex, w_ev = [], None
+        for i in range(n):
+            c0, w = span[i]
+            wait(act, st[i])
+            ex.append(sig(act.activation(T.pT[0:QP, c0:c0 + w], ST[banks[i]][0:QP, 0:w], F.Exp,
+                                         bias=col(T.nm, shift), scale=1.0, accum_out=col(T.sl, lc + i))))
+            if i == 0 and prev is not None:
+                w_ev = sig(act.activation(col(T.sl, wc), col(T.nm, prev["shift"]), F.Exp, bias=col(T.nm, shift), scale=-1.0))
+        total = sum(len(ch) for ch in chunks) + (0 if prev is None else 1)
+        done = [0]
+        o_ev = [None]
+
+        def acc(lhsT, rhs):
+            done[0] += 1
+            ins = pe.matmul(O[0:QP, 0:128], lhsT, rhs, done[0] == 1, done[0] == total)
+            if done[0] == total:
+                o_ev[0] = sig(ins)
+
+        cp = [None] * n
+
+        def turn(i):
+            wait(pe, ex[i])
+            t = sig(*[pe.transpose(PT[banks[i]][:, QP * jj:QP * jj + QP], T.pT[0:QP, 128 * b:128 * b + 128], T.ident[0:QP, :])
+                      for jj, b in enumerate(chunks[i])])
+            wait(dve, t)
+            ch = chunks[i]
+            cp[i] = sig(dve.tensor_copy(T.P[:, QP * ch[0]:QP * (ch[-1] + 1)], PT[banks[i]][:, 0:QP * len(ch)]))
+
+        def pv(i):
+            wait(pe, cp[i])
+            for b in chunks[i]:
+                v_here(b)
+                acc(T.P[:, QP * b:QP * b + QP], T.V[:, 128 * b:128 * b + 128])
+
+        turn(0)
+        if prev is not None:
+            wait(dve, w_ev)
+            d_ev = sig(dve.tensor_scalar(prev["D"][0:QP, :], T.ident[0:QP, :], col(T.sl, wc), None, A.mult))
+            wait(pe, d_ev)
+            wait(pe, prev["o_ev"])
+            acc(prev["D"][0:QP, :], prev["O"][0:QP, :])
+        for i in range(1, n):
+            turn(i)
+            pv(i - 1)
+        pv(n - 1)
+        for e in ex:
+            wait(dve, e)
+        lcol, l_ev = lc, ex[0]
+        if n > 1:
+            lcol = lsum
+            l_ev = sig(dve.tensor_reduce(col(T.sl, lsum), T.sl[0:QP, lc:lc + n], X, A.add))
+            wait(dve, l_ev)
+        if prev is not None:
+            wait(dve, prev["l_ev"])
+            l_ev = sig(dve.tensor_scalar(col(T.sl, Lc), col(T.sl, prev["l"]), col(T.sl, wc), col(T.sl, lcol), A.mult, A.add))
+            lcol = Lc
+        if not last:
+            wait(dve, o_ev[0])
+            Obuf, Dbuf = keep[s]
+            oc = sig(dve.tensor_copy(Obuf[0:QP, :], O[0:QP, 0:128]))
+            prev = {"shift": shift, "shift_ev": shift_ev, "l": lcol, "l_ev": l_ev, "O": Obuf, "D": Dbuf, "o_ev": oc}
+        else:
+            wait(dve, l_ev)
+            r_ev = sig(dve.reciprocal(col(T.sl, rc), col(T.sl, lcol)))
+            wait(dve, r_ev)
+            wait(dve, o_ev[0])
+            y_ev = sig(dve.tensor_scalar(T.ysb[0:QP, :], O[0:QP, 0:128], col(T.sl, rc), None, A.mult))
+            wait(sp, y_ev)
+            sp.dma_start(T.y[:, :], T.ysb[0:QP, :]).then_inc(T.sem.sty, 16)
+            sp.wait_ge(T.sem.sty, 16)
+    for name in sorted(open_ev):
+        if open_ev[name]:
+            wait(g, name)

@@ -1,6 +1,6 @@
 from concourse.mybir import AluOpType, AxisListType, ActivationFunctionType
 
-NEV = 80
+NEV = 96
 ENG_HOP = 8
 ENG_ROOT = 8
 
@@ -79,6 +79,7 @@ def make_plan(T, topo):
                 best, best_cost = c, cost
         relay[r] = best
         busy += links(r, best) + links(best, root)
+    far = sorted(far, key=lambda r: (len(links(r, relay[r])) + len(links(relay[r], root)), len(links(r, relay[r]))))
     return root, direct, far, relay
 
 
@@ -214,16 +215,16 @@ def root_program(g, T, rank_of_slot, stages):
         nmc[0] = shift + 1
         wait(act, shift_ev)
         lc = slc[0]
-        wc, lsum, Lc, rc = lc + n, lc + n + 1, lc + n + 2, lc + n + 3
-        slc[0] = lc + n + 4
+        wc, Lc, rc = lc + n, lc + n + 1, lc + 2 * n + 1
+        slc[0] = lc + 2 * n + 2
         ex, w_ev = [], None
+        if prev is not None:
+            w_ev = sig(act.activation(col(T.sl, wc), col(T.nm, prev["shift"]), F.Exp, bias=col(T.nm, shift), scale=-1.0))
         for i in range(n):
             c0, w = span[i]
             wait(act, st[i])
             ex.append(sig(act.activation(T.pT[0:QP, c0:c0 + w], ST[banks[i]][0:QP, 0:w], F.Exp,
                                          bias=col(T.nm, shift), scale=1.0, accum_out=col(T.sl, lc + i))))
-            if i == 0 and prev is not None:
-                w_ev = sig(act.activation(col(T.sl, wc), col(T.nm, prev["shift"]), F.Exp, bias=col(T.nm, shift), scale=-1.0))
         total = sum(len(ch) for ch in chunks) + (0 if prev is None else 1)
         done = [0]
         o_ev = [None]
@@ -236,10 +237,12 @@ def root_program(g, T, rank_of_slot, stages):
 
         cp = [None] * n
 
-        def turn(i):
+        def turn(i, first=None):
             wait(pe, ex[i])
             t = sig(*[pe.transpose(PT[banks[i]][:, QP * jj:QP * jj + QP], T.pT[0:QP, 128 * b:128 * b + 128], T.ident[0:QP, :])
                       for jj, b in enumerate(chunks[i])])
+            if first is not None:
+                first()
             wait(dve, t)
             ch = chunks[i]
             cp[i] = sig(dve.tensor_copy(T.P[:, QP * ch[0]:QP * (ch[-1] + 1)], PT[banks[i]][:, 0:QP * len(ch)]))
@@ -250,28 +253,48 @@ def root_program(g, T, rank_of_slot, stages):
                 v_here(b)
                 acc(T.P[:, QP * b:QP * b + QP], T.V[:, 128 * b:128 * b + 128])
 
-        turn(0)
-        if prev is not None:
+        lnow = [None, None]
+
+        def lpart(i):
+            wait(dve, ex[i])
+            if i == 0 and prev is None:
+                lnow[0], lnow[1] = lc, ex[0]
+                return
+            if i == 0:
+                wait(dve, w_ev)
+                wait(dve, prev["l_ev"])
+                ins = dve.tensor_scalar(col(T.sl, Lc), col(T.sl, prev["l"]), col(T.sl, wc), col(T.sl, lc), A.mult, A.add)
+            else:
+                wait(dve, lnow[1])
+                ins = dve.tensor_scalar(col(T.sl, Lc + i), col(T.sl, lnow[0]), col(T.sl, lc + i), None, A.add)
+            lnow[0], lnow[1] = Lc + i, sig(ins)
+
+        d_ev = [None]
+
+        def diag():
             wait(dve, w_ev)
-            d_ev = sig(dve.tensor_scalar(prev["D"][0:QP, :], T.ident[0:QP, :], col(T.sl, wc), None, A.mult))
-            wait(pe, d_ev)
+            d_ev[0] = sig(dve.tensor_scalar(prev["D"][0:QP, :], T.ident[0:QP, :], col(T.sl, wc), None, A.mult))
+
+        if prev is None:
+            turn(0)
+        else:
+            turn(0, diag)
+            wait(pe, d_ev[0])
             wait(pe, prev["o_ev"])
             acc(prev["D"][0:QP, :], prev["O"][0:QP, :])
+        if n > 1:
+            lpart(0)
         for i in range(1, n):
-            turn(i)
+            if i == n - 1:
+                turn(i, lambda: lpart(n - 1))
+            else:
+                turn(i)
+                lpart(i)
             pv(i - 1)
         pv(n - 1)
-        for e in ex:
-            wait(dve, e)
-        lcol, l_ev = lc, ex[0]
-        if n > 1:
-            lcol = lsum
-            l_ev = sig(dve.tensor_reduce(col(T.sl, lsum), T.sl[0:QP, lc:lc + n], X, A.add))
-            wait(dve, l_ev)
-        if prev is not None:
-            wait(dve, prev["l_ev"])
-            l_ev = sig(dve.tensor_scalar(col(T.sl, Lc), col(T.sl, prev["l"]), col(T.sl, wc), col(T.sl, lcol), A.mult, A.add))
-            lcol = Lc
+        if n == 1:
+            lpart(0)
+        lcol, l_ev = lnow[0], lnow[1]
         if not last:
             wait(dve, o_ev[0])
             Obuf, Dbuf = keep[s]

from concourse.mybir import AluOpType, AxisListType, ActivationFunctionType

NEV = 96
ENG_HOP = 8
ENG_ROOT = 8

SCRATCH = {
    "stg": ("dram", [2, 128, 128], "bfloat16"),
    "qs": ("sbuf", [128, 64], "bfloat16"),
    "K": ("sbuf", [128, 1024], "bfloat16"),
    "V": ("sbuf", [128, 1024], "bfloat16"),
    "ident": ("sbuf", [128, 64], "bfloat16"),
    "pT": ("sbuf", [128, 1024], "bfloat16"),
    "P": ("sbuf", [128, 512], "bfloat16"),
    "Oa": ("sbuf", [128, 128], "bfloat16"),
    "Ob": ("sbuf", [128, 128], "bfloat16"),
    "Da": ("sbuf", [128, 64], "bfloat16"),
    "Db": ("sbuf", [128, 64], "bfloat16"),
    "nm": ("sbuf", [128, 16], "float32"),
    "sl": ("sbuf", [128, 24], "float32"),
    "ysb": ("sbuf", [128, 128], "bfloat16"),
    "ST0": ("psum", [128, 512], "float32"), "ST1": ("psum", [128, 512], "float32"), "ST2": ("psum", [128, 512], "float32"),
    "PT0": ("psum", [128, 1024], "bfloat16"), "PT1": ("psum", [128, 1024], "bfloat16"), "PT2": ("psum", [128, 1024], "bfloat16"),
    "O0": ("psum", [128, 512], "float32"), "O1": ("psum", [128, 512], "float32"),
}
SEMAPHORES = (["lq", "lk", "lv", "snt", "rk", "rv", "sty"] + ["ka%d" % j for j in range(8)] + ["va%d" % j for j in range(8)]
              + ["e%d" % i for i in range(NEV)])

PLANS = {}


def plan(T, topo):
    if "plan" not in PLANS:
        PLANS["plan"] = make_plan(T, topo)
    return PLANS["plan"]


def make_plan(T, topo):
    group = list(T.cores)
    root = group[T.root]
    per_host = topo.CORES_PER_HOST
    world = range((1 + max(topo.host(c) for c in group)) * per_host)
    mate_of = {}

    def chipof(c):
        return (topo.host(c), topo.chip(c))

    def inrack(a, b):
        if chipof(a) == chipof(b):
            return []
        d = topo.die(a)
        if topo.mates(a, b):
            return [("mate", chipof(a), d)]
        if topo.same_plane(a, b):
            return [("out", chipof(a), d), ("in", chipof(b), d)]
        if chipof(a) not in mate_of:
            mate_of[chipof(a)] = [x for x in world if topo.mates(a, x)][0]
        m = mate_of[chipof(a)]
        return [("mate", chipof(a), d), ("out", chipof(m), d), ("in", chipof(b), d)]

    def links(a, b):
        if topo.rack(topo.host(a)) == topo.rack(topo.host(b)):
            return inrack(a, b)
        shift = (topo.host(b) - topo.host(a)) * per_host
        d = topo.die(a)
        return [("cable", chipof(a), d)] + inrack(a + shift, b) + inrack(a, b - shift) + [("cable", chipof(b - shift), d)]

    direct = [c for c in group if c != root and topo.may_write(c, root)]
    far = [c for c in group if c != root and not topo.may_write(c, root)]
    relay, busy = {}, []
    for r in far:
        cand = [c for c in world if c not in group and c not in relay.values()
                and topo.may_write(r, c) and topo.may_write(c, root)]
        best, best_cost = None, None
        for c in cand:
            way = links(r, c) + links(c, root)
            cost = (len([x for x in way if x in busy]), len(set(way)), topo.die(c) != topo.die(r), -c)
            if best is None or cost < best_cost:
                best, best_cost = c, cost
        relay[r] = best
        busy += links(r, best) + links(best, root)
    far = sorted(far, key=lambda r: (len(links(r, relay[r])) + len(links(relay[r], root)), len(links(r, relay[r]))))
    return root, direct, far, relay


def engines(mask, n):
    out, bit = 0, 1
    while n > 0:
        if mask & bit:
            out |= bit
            n -= 1
        bit <<= 1
    return out


def send(g, T, topo, core, dst, out_ap, in_ap, sem, n):
    rid, pid = topo.addr(dst, core)
    g.remote_dma(out_ap=out_ap, in_ap=in_ap, remote_sem=sem, local_sem=T.sem.snt, pid=pid, routing_id=rid,
                 dma_engine_mask=engines(topo.mask(core, dst), n))


def rank_program(g, core, T, topo):
    root, direct, far, relay = plan(T, topo)
    order = [root] + direct + far
    if core == root:
        n0, n1 = 1, 1 + len(direct)
        late = list(range(n1, len(order)))
        chunks = [late[0:1], late[1:3], late[3:5]]
        root_program(g, T, [T.rank_of(c) for c in order], [[[0]], [list(range(n0, n1))], chunks])
        return
    if core in order:
        b, j = order.index(core), T.rank_of(core)
        g.sync.dma_start(T.stg[0], T.k[:, :]).then_inc(T.sem.lk, 16)
        g.scalar.dma_start(T.stg[1], T.v[:, :]).then_inc(T.sem.lv, 16)
        cols = slice(128 * b, 128 * b + 128)
        if core in direct:
            g.wait_ge(T.sem.lk, 16)
            send(g, T, topo, core, root, T.K[:, cols], T.stg[0], T.sem["ka%d" % j], ENG_ROOT)
            g.wait_ge(T.sem.lv, 16)
            send(g, T, topo, core, root, T.V[:, cols], T.stg[1], T.sem["va%d" % j], ENG_ROOT)
            g.wait_ge(T.sem.snt, 2 * ENG_ROOT)
        else:
            g.wait_ge(T.sem.lk, 16)
            send(g, T, topo, core, relay[core], T.stg[0], T.stg[0], T.sem.rk, ENG_HOP)
            g.wait_ge(T.sem.lv, 16)
            send(g, T, topo, core, relay[core], T.stg[1], T.stg[1], T.sem.rv, ENG_HOP)
            g.wait_ge(T.sem.snt, 2 * ENG_HOP)
        return
    for r in far:
        if relay[r] == core:
            b, j = order.index(r), T.rank_of(r)
            cols = slice(128 * b, 128 * b + 128)
            g.wait_ge(T.sem.rk, ENG_HOP)
            send(g, T, topo, core, root, T.K[:, cols], T.stg[0], T.sem["ka%d" % j], ENG_ROOT)
            g.wait_ge(T.sem.rv, ENG_HOP)
            send(g, T, topo, core, root, T.V[:, cols], T.stg[1], T.sem["va%d" % j], ENG_ROOT)
            g.wait_ge(T.sem.snt, 2 * ENG_ROOT)


def root_program(g, T, rank_of_slot, stages):
    A, X, F = AluOpType, AxisListType.X, ActivationFunctionType
    pe, dve, act, sp = g.tensor, g.vector, g.scalar, g.sync
    ST, PT, OB = [T.ST0, T.ST1, T.ST2], [T.PT0, T.PT1, T.PT2], [T.O0, T.O1]
    QP = 64
    count, need, open_ev = [0], {}, {}

    def sig(*instrs):
        name = "e%d" % count[0]
        count[0] += 1
        for ins in instrs:
            ins.then_inc(T.sem[name], 1)
        need[name] = len(instrs)
        open_ev[name] = True
        return name

    def wait(queue, name):
        queue.wait_ge(T.sem[name], need[name])
        open_ev[name] = False

    def col(t, c):
        return t[0:QP, c:c + 1]

    sp.dma_start(T.qs[:, :], T.q[:, :]).then_inc(T.sem.lq, 16)
    act.dma_start(T.K[:, 0:128], T.k[:, :]).then_inc(T.sem.lk, 16)
    sp.dma_start(T.V[:, 0:128], T.v[:, :]).then_inc(T.sem.lv, 16)
    ones = sig(dve.memset(T.ident[0:QP, :], 1.0))
    wait(g, ones)
    idn = sig(g.affine_select(T.ident[0:QP, :], T.ident[0:QP, :], [[-1, QP]], A.is_equal, 0.0, 0, 1))
    wait(pe, idn)
    wait(dve, idn)
    pe.wait_ge(T.sem.lq, 16)

    def k_here(b):
        if b == 0:
            pe.wait_ge(T.sem.lk, 16)
        else:
            pe.wait_ge(T.sem["ka%d" % rank_of_slot[b]], ENG_ROOT)

    def v_here(b):
        if b == 0:
            pe.wait_ge(T.sem.lv, 16)
        else:
            pe.wait_ge(T.sem["va%d" % rank_of_slot[b]], ENG_ROOT)

    banks_of = [[0], [1], [2, 0, 1]]
    keep = [(T.Oa, T.Da), (T.Ob, T.Db)]
    nmc, slc = [0], [0]
    prev = None
    for s, chunks in enumerate(stages):
        last = s == len(stages) - 1
        banks, n, O = banks_of[s], len(chunks), OB[s % 2]
        span = [(128 * ch[0], 128 * len(ch)) for ch in chunks]
        st = []
        for i, ch in enumerate(chunks):
            for b in ch:
                k_here(b)
            c0, w = span[i]
            st.append(sig(pe.matmul(ST[banks[i]][0:QP, 0:w], T.qs[:, :], T.K[:, c0:c0 + w], True, True)))
        base = nmc[0]
        red = []
        for i in range(n):
            wait(dve, st[i])
            red.append(sig(dve.tensor_reduce(col(T.nm, base + i), ST[banks[i]][0:QP, 0:span[i][1]], X, A.max, negate=True)))
        if prev is None and n == 1:
            shift, shift_ev = base, red[0]
        else:
            for e in red:
                wait(dve, e)
            lo = base
            if prev is not None:
                wait(dve, prev["shift_ev"])
                lo = base - 1
            shift = base + n
            shift_ev = sig(dve.tensor_reduce(col(T.nm, shift), T.nm[0:QP, lo:base + n], X, A.min))
        nmc[0] = shift + 1
        wait(act, shift_ev)
        lc = slc[0]
        wc, Lc, rc = lc + n, lc + n + 1, lc + 2 * n + 1
        slc[0] = lc + 2 * n + 2
        ex, w_ev = [], None
        if prev is not None:
            w_ev = sig(act.activation(col(T.sl, wc), col(T.nm, prev["shift"]), F.Exp, bias=col(T.nm, shift), scale=-1.0))
        for i in range(n):
            c0, w = span[i]
            wait(act, st[i])
            ex.append(sig(act.activation(T.pT[0:QP, c0:c0 + w], ST[banks[i]][0:QP, 0:w], F.Exp,
                                         bias=col(T.nm, shift), scale=1.0, accum_out=col(T.sl, lc + i))))
        total = sum(len(ch) for ch in chunks) + (0 if prev is None else 1)
        done = [0]
        o_ev = [None]

        def acc(lhsT, rhs):
            done[0] += 1
            ins = pe.matmul(O[0:QP, 0:128], lhsT, rhs, done[0] == 1, done[0] == total)
            if done[0] == total:
                o_ev[0] = sig(ins)

        cp = [None] * n

        def turn(i, first=None):
            wait(pe, ex[i])
            t = sig(*[pe.transpose(PT[banks[i]][:, QP * jj:QP * jj + QP], T.pT[0:QP, 128 * b:128 * b + 128], T.ident[0:QP, :])
                      for jj, b in enumerate(chunks[i])])
            if first is not None:
                first()
            wait(dve, t)
            ch = chunks[i]
            cp[i] = sig(dve.tensor_copy(T.P[:, QP * ch[0]:QP * (ch[-1] + 1)], PT[banks[i]][:, 0:QP * len(ch)]))

        def pv(i):
            wait(pe, cp[i])
            for b in chunks[i]:
                v_here(b)
                acc(T.P[:, QP * b:QP * b + QP], T.V[:, 128 * b:128 * b + 128])

        lnow = [None, None]

        def lpart(i):
            wait(dve, ex[i])
            if i == 0 and prev is None:
                lnow[0], lnow[1] = lc, ex[0]
                return
            if i == 0:
                wait(dve, w_ev)
                wait(dve, prev["l_ev"])
                ins = dve.tensor_scalar(col(T.sl, Lc), col(T.sl, prev["l"]), col(T.sl, wc), col(T.sl, lc), A.mult, A.add)
            else:
                wait(dve, lnow[1])
                ins = dve.tensor_scalar(col(T.sl, Lc + i), col(T.sl, lnow[0]), col(T.sl, lc + i), None, A.add)
            lnow[0], lnow[1] = Lc + i, sig(ins)

        d_ev = [None]

        def diag():
            wait(dve, w_ev)
            d_ev[0] = sig(dve.tensor_scalar(prev["D"][0:QP, :], T.ident[0:QP, :], col(T.sl, wc), None, A.mult))

        if prev is None:
            turn(0)
        else:
            turn(0, diag)
            wait(pe, d_ev[0])
            wait(pe, prev["o_ev"])
            acc(prev["D"][0:QP, :], prev["O"][0:QP, :])
        if n > 1:
            lpart(0)
        for i in range(1, n):
            if i == n - 1:
                turn(i, lambda: lpart(n - 1))
            else:
                turn(i)
                lpart(i)
            pv(i - 1)
        pv(n - 1)
        if n == 1:
            lpart(0)
        lcol, l_ev = lnow[0], lnow[1]
        if not last:
            wait(dve, o_ev[0])
            Obuf, Dbuf = keep[s]
            oc = sig(dve.tensor_copy(Obuf[0:QP, :], O[0:QP, 0:128]))
            prev = {"shift": shift, "shift_ev": shift_ev, "l": lcol, "l_ev": l_ev, "O": Obuf, "D": Dbuf, "o_ev": oc}
        else:
            wait(dve, l_ev)
            r_ev = sig(dve.reciprocal(col(T.sl, rc), col(T.sl, lcol)))
            wait(dve, r_ev)
            wait(dve, o_ev[0])
            y_ev = sig(dve.tensor_scalar(T.ysb[0:QP, :], O[0:QP, 0:128], col(T.sl, rc), None, A.mult))
            wait(sp, y_ev)
            sp.dma_start(T.y[:, :], T.ysb[0:QP, :]).then_inc(T.sem.sty, 16)
            sp.wait_ge(T.sem.sty, 16)
    for name in sorted(open_ev):
        if open_ev[name]:
            wait(g, name)
